import numpy as np, ml_dtypes
CORES = [24,48,72,152,176,200]
N = 6
import mx_ref
NC, G = 192, 4
C = np.float32(0.019)
WID = [192,128,192,160,160,192]
BF = ml_dtypes.bfloat16
def cut(t, i, w=512):
    return t[:, w * i:w * i + w]
def tile(rs):
    return np.stack(rs, axis=2).reshape(128, -1).astype(BF)
def layer(w, X):
    out = []
    for i in range(G):
        for t in range(len(X)):
            p = mx_ref.matmul(mx_ref.quantize(cut(w, len(X) * i + t)), X[t])
            z = p if t == 0 else z + p
        out.append(z)
    return out
def act(Z):
    return [np.maximum(z, 0) * C for z in Z]
def setup_inputs(rng):
    def f(*shape):
        return mx_ref.flush((rng.standard_normal(shape, dtype=np.float32) * np.exp2(rng.integers(-2, 3, shape[:-1] + (1,)))).astype(BF))
    return {"x": f(N, 128, 4 * NC), "w1": f(N, 128, G * 512), "w2": f(N, 128, 512)}
def setup_inputs_blocks(rng):
    d = setup_inputs(rng)
    for k in ("x", "w1", "w2"): d[k] = mx_ref.spread(d[k], rng, 2)
    return d
def setup_inputs_wide(rng):
    d = setup_inputs(rng)
    for k in ("x", "w1", "w2"): d[k] = mx_ref.flush((d[k].astype(np.float32) * np.exp2(rng.integers(-6, 7, (N, 1, 1))).astype(np.float32)).astype(BF))
    return d
def reference(x, w1, w2):
    X = [mx_ref.quantize(x[j][:, :4 * WID[j]]) for j in range(N)]
    y = np.full((N, 128, NC), np.nan, np.float32)
    for c in range(N):
        for r in range(N):
            p = mx_ref.matmul(mx_ref.quantize(w2[r]), mx_ref.quantize(tile(act(layer(w1[r], [X[c]])))))
            z = p if r == 0 else z + p
        y[c][:, :WID[c]] = z
    return {"y": y}

@@ -1,0 +1,274 @@
+from concourse.bass import DstId, RemoteDMATransfer
+from concourse.mybir import dt, AluOpType, ActivationFunctionType
+
+NC, G, TW, SIM = 192, 4, 128, 256
+C = 0.019
+NZ = 5
+
+SCRATCH = {
+    "xin": ("sbuf", [128, 4 * NC], "bfloat16"),
+    "w1in": ("sbuf", [128, G * 512], "bfloat16"),
+    "w2in": ("sbuf", [128, 512], "bfloat16"),
+    "xq": ("sbuf", [128, 512], "float8_e4m3fn_x4"),
+    "xs": ("sbuf", [128, 512], "uint8"),
+    "wq": ("sbuf", [128, 10 * TW], "float8_e4m3fn_x4"),
+    "ws": ("sbuf", [128, 10 * TW], "uint8"),
+    "h": ("sbuf", [128, 6 * 4 * NC], "bfloat16"),
+    "hq": ("sbuf", [128, 6 * NC], "float8_e4m3fn_x4"),
+    "hs": ("sbuf", [128, 6 * NC], "uint8"),
+    "ysend": ("sbuf", [128, 3 * NC], "float32"),
+    "yland": ("sbuf", [128, 3 * NC], "float32"),
+    "yacc": ("sbuf", [128, NC], "float32"),
+    "yout": ("sbuf", [128, NC], "float32"),
+    "rxq": ("sbuf", [128, NC], "float8_e4m3fn_x4"),
+    "rxs": ("sbuf", [128, NC], "uint8"),
+    "rwq": ("sbuf", [128, 2 * TW], "float8_e4m3fn_x4"),
+    "ry": ("sbuf", [128, NC], "float32"),
+    "z": ("psum", [128, 512 * NZ], "float32"),
+    "yp": ("psum", [128, 512 * 3], "float32"),
+}
+SEMAPHORES = ["ldx", "ldwa", "ldwb", "ldw2", "pe", "ac", "dv", "xa0", "xa1", "xa2", "wa", "wb", "ya0", "ya1", "ya2", "ls", "st",
+              "f0", "f1", "f2"]
+
+
+def bits(m):
+    return [e for e in range(16) if m >> e & 1]
+
+
+def mask_of(es):
+    return sum(1 << e for e in es)
+
+
+def layout(R, T, topo):
+    grp = [c for c in T.cores if topo.host(c) == topo.host(R)]
+    partner = [c for c in T.cores if topo.host(c) != topo.host(R) and topo.chip(c) == topo.chip(R)][0]
+    cross = [c for c in grp if c != R and not topo.may_write(R, c)]
+    direct = [c for c in grp if c != R and topo.may_write(R, c)]
+    mine = [c for c in range(SIM) if c != R and topo.host(c) == topo.host(R) and topo.chip(c) == topo.chip(R)]
+    own = [h for h in mine if topo.may_write(h, cross[0])]
+    rest = [h for h in mine if h not in own]
+    far = [h for h in own if topo.die(h) != topo.die(R)]
+    near = [h for h in own if topo.die(h) == topo.die(R)]
+    if len(cross) == 1:
+        rel = {cross[0]: far if grp.index(R) < grp.index(cross[0]) else near}
+    else:
+        rel = {cross[0]: far, cross[1]: near}
+    return {"grp": grp, "partner": partner, "cross": cross, "direct": direct, "rel": rel,
+            "pfar": [h for h in rest if topo.die(h) != topo.die(R)], "pnear": [h for h in rest if topo.die(h) == topo.die(R)]}
+
+
+def rank_program(g, core, T, topo):
+    WID = T.tables["WID"]
+    wid = {c: WID[T.rank_of(c)] for c in T.cores}
+    u8 = dt.uint8
+    S = T.sem
+    home = [c for c in T.cores if topo.host(c) == topo.host(core) and topo.chip(c) == topo.chip(core)]
+    if not home:
+        return
+    R = home[0]
+    L = layout(R, T, topo)
+    grp, partner = L["grp"], L["partner"]
+    off, k = {}, 0
+    for c in grp:
+        off[c] = k
+        k += wid[c]
+    n, me = wid[R], grp.index(R)
+    codes = lambda buf, a, b: buf[:, a:b].bitcast(u8)
+
+    jobs = []
+    for D in L["cross"]:
+        r = L["rel"][D]
+        jobs.append(("xq", r[0], D, codes(T.rxq, 0, n), codes(T.xq, off[R], off[R] + n), S["xa%d" % me]))
+        jobs.append(("xs", r[1], D, T.rxs[:, 0:n], T.xs[:, off[R]:off[R] + n], S["xa%d" % me]))
+    wroute = {0: (L["pfar"][0], 0), 1: (L["pfar"][1], 0), 2: (L["pnear"][0], 0), 4: (L["pfar"][0], 1)}
+    for i in (0, 1, 2, 4):
+        h, s = wroute[i]
+        jobs.append((i, h, partner, codes(T.rwq, s * TW, s * TW + TW), codes(T.wq, (5 + i) * TW, (6 + i) * TW), S.wb if i == 4 else S.wa))
+    for D in L["cross"]:
+        m = wid[D]
+        jobs.append(("y", L["rel"][D][0], D, T.ry[:, 0:m], T.yland[:, me * NC:me * NC + m], S["ya%d" % me]))
+    slot, count = {}, {}
+    for what, h, D, _a, _b, _s in jobs:
+        slot[(what, D, h)] = count.get(h, 0)
+        count[h] = count.get(h, 0) + 1
+
+    def land(what, D):
+        for w, h, d, a, _b, _s in jobs:
+            if w == what and d == D:
+                return h, a, S["f%d" % slot[(w, d, h)]]
+
+    eoff = bits(topo.mask(R, partner))
+    eon = bits(topo.mask(R, L["pnear"][0]))
+    ein = [e for e in eon if e not in eoff]
+    half = len(ein) // 2
+    if L["direct"]:
+        xeng = {L["cross"][0]: ein}
+    else:
+        xeng = {L["cross"][0]: ein, L["cross"][1]: eoff}
+    weng = {0: ein[:half], 1: ein[half:], 2: ein[:half], 4: ein[half:]}
+
+    if core != R:
+        sent = 0
+        for what, h, D, a, b, s in jobs:
+            if h != core:
+                continue
+            got = xeng[D] if what in ("xq", "xs") else eon if what == "y" else weng[what]
+            g.wait_ge(S["f%d" % slot[(what, D, h)]], len(got))
+            m = topo.mask(core, D)
+            rid, pid = topo.addr(D, core)
+            g.remote_dma(b, a, s, S.ls, pid, rid, m)
+            sent += len(bits(m))
+        if sent:
+            g.wait_ge(S.ls, sent)
+        return
+
+    q = {"pe": g.tensor, "ac": g.scalar, "dv": g.vector, "g": g, "sy": g.sync}
+    cnt, seen, sent = {"pe": 0, "ac": 0, "dv": 0}, {}, [0]
+
+    def done(sem, ins):
+        ins.then_inc(S[sem], 1)
+        cnt[sem] += 1
+        return (sem, cnt[sem])
+
+    def wait(queue, *evs):
+        for sem, v in evs:
+            if seen.get((queue, sem), 0) < v:
+                q[queue].wait_ge(S[sem], v)
+                seen[(queue, sem)] = v
+
+    def tr(dst, src, out, es, sem):
+        rid, pid = topo.addr(dst, core)
+        return RemoteDMATransfer(dst_ids=[DstId(rid=rid, pnc=pid)], dma_engine_mask=mask_of(es), remote_sem=sem, src=src, dst=out)
+
+    def send(trs, engines):
+        g.remote_dma_fused(trs, local_sem=S.ls)
+        sent[0] += engines
+
+    g.sync.dma_start(T.xin[:, :4 * n], T.x[:, :4 * n]).then_inc(S.ldx, 16)
+    g.sync.dma_start(T.w1in[:, :1024], T.w1[:, :1024]).then_inc(S.ldwa, 16)
+    g.sync.dma_start(T.w1in[:, 1024:], T.w1[:, 1024:]).then_inc(S.ldwb, 16)
+    g.sync.dma_start(T.w2in[:], T.w2[:]).then_inc(S.ldw2, 16)
+
+    o = off[R]
+    wait("dv", ("ldx", 16))
+    qx = done("dv", g.vector.quantize_mx(T.xq[:, o:o + n], T.xs[:, o:o + n], T.xin[:, :4 * n]))
+    qw = []
+    for i in range(G):
+        wait("dv", ("ldwa" if i < 2 else "ldwb", 16))
+        qw.append(done("dv", g.vector.quantize_mx(T.wq[:, i * TW:(i + 1) * TW], T.ws[:, i * TW:(i + 1) * TW], T.w1in[:, 512 * i:512 * i + 512])))
+    wait("dv", ("ldw2", 16))
+    qw.append(done("dv", g.vector.quantize_mx(T.wq[:, 4 * TW:5 * TW], T.ws[:, 4 * TW:5 * TW], T.w2in[:])))
+
+    wait("g", qx)
+    for what in ("xq", "xs"):
+        src = codes(T.xq, o, o + n) if what == "xq" else T.xs[:, o:o + n]
+        trs, ne = [], 0
+        for D in L["cross"]:
+            h, a, s = land(what, D)
+            trs.append(tr(h, src, a, xeng[D], s))
+            ne += len(xeng[D])
+        for D in L["direct"]:
+            trs.append(tr(D, src, src, eoff, S["xa%d" % me]))
+            ne += len(eoff)
+        send(trs, ne)
+
+    def wrelay(tiles):
+        trs = []
+        for i in tiles:
+            h, a, s = land(i, partner)
+            trs.append(tr(h, codes(T.wq, i * TW, (i + 1) * TW), a, weng[i], s))
+        send(trs, sum(len(weng[i]) for i in tiles))
+
+    wait("g", qw[1])
+    wrelay((0, 1))
+    wait("g", qw[3])
+    send([tr(partner, codes(T.wq, 3 * TW, 4 * TW), codes(T.wq, 8 * TW, 9 * TW), eoff, S.wa)], len(eoff))
+    wait("g", qw[4])
+    send([tr(partner, T.ws[:, 0:5 * TW], T.ws[:, 5 * TW:10 * TW], eoff, S.wa)], len(eoff))
+    wrelay((2, 4))
+
+    ne = len(eoff)
+    xarr = {c: ("xa%d" % grp.index(c), 2 * ne) for c in grp if c != R}
+    yarr = {c: ("ya%d" % grp.index(c), ne) for c in grp if c != R}
+    wall, w2all = ("wa", 5 * ne), ("wb", ne)
+
+    pieces = [(0, c) for c in [R] + L["direct"] + L["cross"]] + [(1, c) for c in L["cross"] + L["direct"] + [R]]
+    P = len(pieces)
+    zfree, zdone, hdone, relu, hq, yfin, ycp = {}, {}, {}, {}, {}, {}, {}
+
+    def mm1(p, b):
+        w, c = pieces[p]
+        m, t, bank = wid[c], 5 * w + b, (4 * p + b) % NZ
+        wait("pe", xarr[c] if c != R else qx, wall if w else qw[b])
+        if bank in zfree:
+            wait("pe", zfree[bank])
+        zdone[(p, b)] = done("pe", g.tensor.matmul_mx(
+            T.z[:, 512 * bank:512 * bank + m], T.wq[:, t * TW:(t + 1) * TW], T.ws[:, t * TW:(t + 1) * TW],
+            T.xq[:, off[c]:off[c] + m], T.xs[:, off[c]:off[c] + m], True, True))
+
+    def mm2(p):
+        w, c = pieces[p]
+        m, t, y = wid[c], 5 * w + 4, 512 * grp.index(c)
+        wait("pe", hq[p], w2all if w else qw[4])
+        yfin[p] = done("pe", g.tensor.matmul_mx(
+            T.yp[:, y:y + m], T.wq[:, t * TW:(t + 1) * TW], T.ws[:, t * TW:(t + 1) * TW],
+            T.hq[:, p * NC:p * NC + m], T.hs[:, p * NC:p * NC + m], w == 0, w == 1))
+
+    def act(p, b):
+        m, bank = wid[pieces[p][1]], (4 * p + b) % NZ
+        out, src = T.h[:, 4 * NC * p + b:4 * NC * p + 4 * m:4], T.z[:, 512 * bank:512 * bank + m]
+        if b in ((0, 1, 2) if p == 0 else (0, 2)):
+            wait("ac", zdone[(p, b)])
+            e = done("ac", g.scalar.activation(out, src, ActivationFunctionType.Relu, scale=C))
+        else:
+            wait("dv", zdone[(p, b)])
+            e = done("dv", g.vector.tensor_scalar(out, src, 0.0, C, AluOpType.max, AluOpType.mult))
+        relu[(p, b)] = zfree[bank] = e
+
+    def quant(p):
+        m = wid[pieces[p][1]]
+        wait("dv", *[relu[(p, b)] for b in range(G)])
+        hq[p] = done("dv", g.vector.quantize_mx(T.hq[:, p * NC:p * NC + m], T.hs[:, p * NC:p * NC + m],
+                                                T.h[:, 4 * NC * p:4 * NC * p + 4 * m]))
+
+    def ycopy(p):
+        w, c = pieces[p]
+        if w == 0 or c == R:
+            return
+        m, k = wid[c], grp.index(c)
+        wait("ac", yfin[p])
+        e = done("ac", g.scalar.activation(T.ysend[:, k * NC:k * NC + m], T.yp[:, 512 * k:512 * k + m], ActivationFunctionType.Copy))
+        wait("g", e)
+        src = T.ysend[:, k * NC:k * NC + m]
+        if c in L["cross"]:
+            h, a, s = land("y", c)
+            send([tr(h, src, a, eon, s)], len(eon))
+        else:
+            send([tr(c, src, T.yland[:, me * NC:me * NC + m], eoff, S["ya%d" % me])], len(eoff))
+
+    for p in range(P):
+        mm1(p, 0)
+        act(p, 0)
+        mm1(p, 1)
+        act(p, 1)
+        if p:
+            mm2(p - 1)
+            ycopy(p - 1)
+        mm1(p, 2)
+        act(p, 2)
+        mm1(p, 3)
+        act(p, 3)
+        quant(p)
+    mm2(P - 1)
+
+    first, last = (L["direct"] + L["cross"])[:2]
+    wait("dv", yfin[P - 1], yarr[first])
+    k = grp.index(first)
+    e = done("dv", g.vector.tensor_tensor(T.yacc[:, :n], T.yp[:, 512 * me:512 * me + n], T.yland[:, k * NC:k * NC + n], AluOpType.add))
+    wait("dv", e, yarr[last])
+    k = grp.index(last)
+    e = done("dv", g.vector.tensor_tensor(T.yout[:, :n], T.yacc[:, :n], T.yland[:, k * NC:k * NC + n], AluOpType.add))
+    wait("sy", e)
+    g.sync.dma_start(T.y[:, :n], T.yout[:, :n]).then_inc(S.st, 16)
+    g.wait_ge(S.ls, sent[0])
+    g.sync.wait_ge(S.st, 16)

@@ -22,7 +22,7 @@ SCRATCH = {
     "yout": ("sbuf", [128, NC], "float32"),
     "rxq": ("sbuf", [128, NC], "float8_e4m3fn_x4"),
     "rxs": ("sbuf", [128, NC], "uint8"),
-    "rwq": ("sbuf", [128, 2 * TW], "float8_e4m3fn_x4"),
+    "rwq": ("sbuf", [128, TW], "float8_e4m3fn_x4"),
     "ry": ("sbuf", [128, NC], "float32"),
     "z": ("psum", [128, 512 * NZ], "float32"),
     "yp": ("psum", [128, 512 * 3], "float32"),
@@ -80,10 +80,8 @@ def rank_program(g, core, T, topo):
         r = L["rel"][D]
         jobs.append(("xq", r[0], D, codes(T.rxq, 0, n), codes(T.xq, off[R], off[R] + n), S["xa%d" % me]))
         jobs.append(("xs", r[1], D, T.rxs[:, 0:n], T.xs[:, off[R]:off[R] + n], S["xa%d" % me]))
-    wroute = {0: (L["pfar"][0], 0), 1: (L["pfar"][1], 0), 2: (L["pnear"][0], 0), 4: (L["pfar"][0], 1)}
-    for i in (0, 1, 2, 4):
-        h, s = wroute[i]
-        jobs.append((i, h, partner, codes(T.rwq, s * TW, s * TW + TW), codes(T.wq, (5 + i) * TW, (6 + i) * TW), S.wb if i == 4 else S.wa))
+    for i, h in ((0, L["pfar"][0]), (1, L["pnear"][0]), (4, L["pfar"][1])):
+        jobs.append((i, h, partner, codes(T.rwq, 0, TW), codes(T.wq, (5 + i) * TW, (6 + i) * TW), S.wb if i == 4 else S.wa))
     for D in L["cross"]:
         m = wid[D]
         jobs.append(("y", L["rel"][D][0], D, T.ry[:, 0:m], T.yland[:, me * NC:me * NC + m], S["ya%d" % me]))
@@ -105,7 +103,7 @@ def rank_program(g, core, T, topo):
         xeng = {L["cross"][0]: ein}
     else:
         xeng = {L["cross"][0]: ein, L["cross"][1]: eoff}
-    weng = {0: ein[:half], 1: ein[half:], 2: ein[:half], 4: ein[half:]}
+    weng = {0: ein[:half], 1: ein[half:], 4: ein}
 
     if core != R:
         sent = 0
@@ -140,9 +138,14 @@ def rank_program(g, core, T, topo):
         rid, pid = topo.addr(dst, core)
         return RemoteDMATransfer(dst_ids=[DstId(rid=rid, pnc=pid)], dma_engine_mask=mask_of(es), remote_sem=sem, src=src, dst=out)
 
-    def send(trs, engines):
-        g.remote_dma_fused(trs, local_sem=S.ls)
-        sent[0] += engines
+    def send(*parts):
+        if parts:
+            g.remote_dma_fused([tr(*p) for p in parts], local_sem=S.ls)
+            sent[0] += sum(len(p[3]) for p in parts)
+
+    def relay(what, D, src, es):
+        h, a, s = land(what, D)
+        return (h, src, a, es, s)
 
     g.sync.dma_start(T.xin[:, :4 * n], T.x[:, :4 * n]).then_inc(S.ldx, 16)
     g.sync.dma_start(T.w1in[:, :1024], T.w1[:, :1024]).then_inc(S.ldwa, 16)
@@ -160,41 +163,28 @@ def rank_program(g, core, T, topo):
     qw.append(done("dv", g.vector.quantize_mx(T.wq[:, 4 * TW:5 * TW], T.ws[:, 4 * TW:5 * TW], T.w2in[:])))
 
     wait("g", qx)
-    for what in ("xq", "xs"):
-        src = codes(T.xq, o, o + n) if what == "xq" else T.xs[:, o:o + n]
-        trs, ne = [], 0
-        for D in L["cross"]:
-            h, a, s = land(what, D)
-            trs.append(tr(h, src, a, xeng[D], s))
-            ne += len(xeng[D])
-        for D in L["direct"]:
-            trs.append(tr(D, src, src, eoff, S["xa%d" % me]))
-            ne += len(eoff)
-        send(trs, ne)
+    mq, ms, sx = codes(T.xq, o, o + n), T.xs[:, o:o + n], S["xa%d" % me]
+    send(*[relay("xq", D, mq, xeng[D]) for D in L["cross"]])
+    send(*([relay("xs", D, ms, xeng[D]) for D in L["cross"]] + [(D, ms, ms, eoff, sx) for D in L["direct"]]))
+    send(*[(D, mq, mq, eoff, sx) for D in L["direct"]])
 
-    def wrelay(tiles):
-        trs = []
-        for i in tiles:
-            h, a, s = land(i, partner)
-            trs.append(tr(h, codes(T.wq, i * TW, (i + 1) * TW), a, weng[i], s))
-        send(trs, sum(len(weng[i]) for i in tiles))
-
+    wcode = lambda a, b: codes(T.wq, a * TW, b * TW)
     wait("g", qw[1])
-    wrelay((0, 1))
+    send(*[relay(i, partner, wcode(i, i + 1), weng[i]) for i in (0, 1)])
     wait("g", qw[3])
-    send([tr(partner, codes(T.wq, 3 * TW, 4 * TW), codes(T.wq, 8 * TW, 9 * TW), eoff, S.wa)], len(eoff))
+    send((partner, wcode(2, 4), wcode(7, 9), eoff, S.wa))
     wait("g", qw[4])
-    send([tr(partner, T.ws[:, 0:5 * TW], T.ws[:, 5 * TW:10 * TW], eoff, S.wa)], len(eoff))
-    wrelay((2, 4))
+    send((partner, T.ws[:, 0:5 * TW], T.ws[:, 5 * TW:10 * TW], eoff, S.wa))
+    send(relay(4, partner, wcode(4, 5), weng[4]))
 
     ne = len(eoff)
     xarr = {c: ("xa%d" % grp.index(c), 2 * ne) for c in grp if c != R}
     yarr = {c: ("ya%d" % grp.index(c), ne) for c in grp if c != R}
-    wall, w2all = ("wa", 5 * ne), ("wb", ne)
+    wall, w2all = ("wa", 4 * ne), ("wb", ne)
 
     pieces = [(0, c) for c in [R] + L["direct"] + L["cross"]] + [(1, c) for c in L["cross"] + L["direct"] + [R]]
     P = len(pieces)
-    zfree, zdone, hdone, relu, hq, yfin, ycp = {}, {}, {}, {}, {}, {}, {}
+    zfree, zdone, relu, hq, yfin = {}, {}, {}, {}, {}
 
     def mm1(p, b):
         w, c = pieces[p]
@@ -241,23 +231,17 @@ def rank_program(g, core, T, topo):
         wait("g", e)
         src = T.ysend[:, k * NC:k * NC + m]
         if c in L["cross"]:
-            h, a, s = land("y", c)
-            send([tr(h, src, a, eon, s)], len(eon))
+            send(relay("y", c, src, eon))
         else:
-            send([tr(c, src, T.yland[:, me * NC:me * NC + m], eoff, S["ya%d" % me])], len(eoff))
+            send((c, src, T.yland[:, me * NC:me * NC + m], eoff, S["ya%d" % me]))
 
     for p in range(P):
-        mm1(p, 0)
-        act(p, 0)
-        mm1(p, 1)
-        act(p, 1)
+        for b in range(G):
+            mm1(p, b)
+            act(p, b)
         if p:
             mm2(p - 1)
             ycopy(p - 1)
-        mm1(p, 2)
-        act(p, 2)
-        mm1(p, 3)
-        act(p, 3)
         quant(p)
     mm2(P - 1)
 

from concourse.bass import DstId, RemoteDMATransfer
from concourse.mybir import dt, AluOpType, ActivationFunctionType

NC, G, TW, SIM = 192, 4, 128, 256
C = 0.019
NZ = 5

SCRATCH = {
    "xin": ("sbuf", [128, 4 * NC], "bfloat16"),
    "w1in": ("sbuf", [128, G * 512], "bfloat16"),
    "w2in": ("sbuf", [128, 512], "bfloat16"),
    "xq": ("sbuf", [128, 512], "float8_e4m3fn_x4"),
    "xs": ("sbuf", [128, 512], "uint8"),
    "wq": ("sbuf", [128, 10 * TW], "float8_e4m3fn_x4"),
    "ws": ("sbuf", [128, 10 * TW], "uint8"),
    "h": ("sbuf", [128, 6 * 4 * NC], "bfloat16"),
    "hq": ("sbuf", [128, 6 * NC], "float8_e4m3fn_x4"),
    "hs": ("sbuf", [128, 6 * NC], "uint8"),
    "ysend": ("sbuf", [128, 3 * NC], "float32"),
    "yland": ("sbuf", [128, 3 * NC], "float32"),
    "yacc": ("sbuf", [128, NC], "float32"),
    "yout": ("sbuf", [128, NC], "float32"),
    "rxq": ("sbuf", [128, NC], "float8_e4m3fn_x4"),
    "rxs": ("sbuf", [128, NC], "uint8"),
    "rwq": ("sbuf", [128, TW], "float8_e4m3fn_x4"),
    "ry": ("sbuf", [128, NC], "float32"),
    "z": ("psum", [128, 512 * NZ], "float32"),
    "yp": ("psum", [128, 512 * 3], "float32"),
}
SEMAPHORES = ["ldx", "ldwa", "ldwb", "ldw2", "pe", "ac", "dv", "xa0", "xa1", "xa2", "wa", "wb", "ya0", "ya1", "ya2", "ls", "st",
              "f0", "f1", "f2"]


def bits(m):
    return [e for e in range(16) if m >> e & 1]


def mask_of(es):
    return sum(1 << e for e in es)


def layout(R, T, topo):
    grp = [c for c in T.cores if topo.host(c) == topo.host(R)]
    partner = [c for c in T.cores if topo.host(c) != topo.host(R) and topo.chip(c) == topo.chip(R)][0]
    cross = [c for c in grp if c != R and not topo.may_write(R, c)]
    direct = [c for c in grp if c != R and topo.may_write(R, c)]
    mine = [c for c in range(SIM) if c != R and topo.host(c) == topo.host(R) and topo.chip(c) == topo.chip(R)]
    own = [h for h in mine if topo.may_write(h, cross[0])]
    rest = [h for h in mine if h not in own]
    far = [h for h in own if topo.die(h) != topo.die(R)]
    near = [h for h in own if topo.die(h) == topo.die(R)]
    if len(cross) == 1:
        rel = {cross[0]: far if grp.index(R) < grp.index(cross[0]) else near}
    else:
        rel = {cross[0]: far, cross[1]: near}
    return {"grp": grp, "partner": partner, "cross": cross, "direct": direct, "rel": rel,
            "pfar": [h for h in rest if topo.die(h) != topo.die(R)], "pnear": [h for h in rest if topo.die(h) == topo.die(R)]}


def rank_program(g, core, T, topo):
    WID = T.tables["WID"]
    wid = {c: WID[T.rank_of(c)] for c in T.cores}
    u8 = dt.uint8
    S = T.sem
    home = [c for c in T.cores if topo.host(c) == topo.host(core) and topo.chip(c) == topo.chip(core)]
    if not home:
        return
    R = home[0]
    L = layout(R, T, topo)
    grp, partner = L["grp"], L["partner"]
    off, k = {}, 0
    for c in grp:
        off[c] = k
        k += wid[c]
    n, me = wid[R], grp.index(R)
    codes = lambda buf, a, b: buf[:, a:b].bitcast(u8)

    jobs = []
    for D in L["cross"]:
        r = L["rel"][D]
        jobs.append(("xq", r[0], D, codes(T.rxq, 0, n), codes(T.xq, off[R], off[R] + n), S["xa%d" % me]))
        jobs.append(("xs", r[1], D, T.rxs[:, 0:n], T.xs[:, off[R]:off[R] + n], S["xa%d" % me]))
    for i, h in ((0, L["pfar"][0]), (1, L["pnear"][0]), (4, L["pfar"][1])):
        jobs.append((i, h, partner, codes(T.rwq, 0, TW), codes(T.wq, (5 + i) * TW, (6 + i) * TW), S.wb if i == 4 else S.wa))
    for D in L["cross"]:
        m = wid[D]
        jobs.append(("y", L["rel"][D][0], D, T.ry[:, 0:m], T.yland[:, me * NC:me * NC + m], S["ya%d" % me]))
    slot, count = {}, {}
    for what, h, D, _a, _b, _s in jobs:
        slot[(what, D, h)] = count.get(h, 0)
        count[h] = count.get(h, 0) + 1

    def land(what, D):
        for w, h, d, a, _b, _s in jobs:
            if w == what and d == D:
                return h, a, S["f%d" % slot[(w, d, h)]]

    eoff = bits(topo.mask(R, partner))
    eon = bits(topo.mask(R, L["pnear"][0]))
    ein = [e for e in eon if e not in eoff]
    half = len(ein) // 2
    if L["direct"]:
        xeng = {L["cross"][0]: ein}
    else:
        xeng = {L["cross"][0]: ein, L["cross"][1]: eoff}
    weng = {0: ein[:half], 1: ein[half:], 4: ein}

    if core != R:
        sent = 0
        for what, h, D, a, b, s in jobs:
            if h != core:
                continue
            got = xeng[D] if what in ("xq", "xs") else eon if what == "y" else weng[what]
            g.wait_ge(S["f%d" % slot[(what, D, h)]], len(got))
            m = topo.mask(core, D)
            rid, pid = topo.addr(D, core)
            g.remote_dma(b, a, s, S.ls, pid, rid, m)
            sent += len(bits(m))
        if sent:
            g.wait_ge(S.ls, sent)
        return

    q = {"pe": g.tensor, "ac": g.scalar, "dv": g.vector, "g": g, "sy": g.sync}
    cnt, seen, sent = {"pe": 0, "ac": 0, "dv": 0}, {}, [0]

    def done(sem, ins):
        ins.then_inc(S[sem], 1)
        cnt[sem] += 1
        return (sem, cnt[sem])

    def wait(queue, *evs):
        for sem, v in evs:
            if seen.get((queue, sem), 0) < v:
                q[queue].wait_ge(S[sem], v)
                seen[(queue, sem)] = v

    def tr(dst, src, out, es, sem):
        rid, pid = topo.addr(dst, core)
        return RemoteDMATransfer(dst_ids=[DstId(rid=rid, pnc=pid)], dma_engine_mask=mask_of(es), remote_sem=sem, src=src, dst=out)

    def send(*parts):
        if parts:
            g.remote_dma_fused([tr(*p) for p in parts], local_sem=S.ls)
            sent[0] += sum(len(p[3]) for p in parts)

    def relay(what, D, src, es):
        h, a, s = land(what, D)
        return (h, src, a, es, s)

    g.sync.dma_start(T.xin[:, :4 * n], T.x[:, :4 * n]).then_inc(S.ldx, 16)
    g.sync.dma_start(T.w1in[:, :1024], T.w1[:, :1024]).then_inc(S.ldwa, 16)
    g.sync.dma_start(T.w1in[:, 1024:], T.w1[:, 1024:]).then_inc(S.ldwb, 16)
    g.sync.dma_start(T.w2in[:], T.w2[:]).then_inc(S.ldw2, 16)

    o = off[R]
    wait("dv", ("ldx", 16))
    qx = done("dv", g.vector.quantize_mx(T.xq[:, o:o + n], T.xs[:, o:o + n], T.xin[:, :4 * n]))
    qw = []
    for i in range(G):
        wait("dv", ("ldwa" if i < 2 else "ldwb", 16))
        qw.append(done("dv", g.vector.quantize_mx(T.wq[:, i * TW:(i + 1) * TW], T.ws[:, i * TW:(i + 1) * TW], T.w1in[:, 512 * i:512 * i + 512])))
    wait("dv", ("ldw2", 16))
    qw.append(done("dv", g.vector.quantize_mx(T.wq[:, 4 * TW:5 * TW], T.ws[:, 4 * TW:5 * TW], T.w2in[:])))

    wait("g", qx)
    mq, ms, sx = codes(T.xq, o, o + n), T.xs[:, o:o + n], S["xa%d" % me]
    send(*[relay("xq", D, mq, xeng[D]) for D in L["cross"]])
    send(*([relay("xs", D, ms, xeng[D]) for D in L["cross"]] + [(D, ms, ms, eoff, sx) for D in L["direct"]]))
    send(*[(D, mq, mq, eoff, sx) for D in L["direct"]])

    wcode = lambda a, b: codes(T.wq, a * TW, b * TW)
    wait("g", qw[1])
    send(*[relay(i, partner, wcode(i, i + 1), weng[i]) for i in (0, 1)])
    wait("g", qw[3])
    send((partner, wcode(2, 4), wcode(7, 9), eoff, S.wa))
    wait("g", qw[4])
    send((partner, T.ws[:, 0:5 * TW], T.ws[:, 5 * TW:10 * TW], eoff, S.wa))
    send(relay(4, partner, wcode(4, 5), weng[4]))

    ne = len(eoff)
    xarr = {c: ("xa%d" % grp.index(c), 2 * ne) for c in grp if c != R}
    yarr = {c: ("ya%d" % grp.index(c), ne) for c in grp if c != R}
    wall, w2all = ("wa", 4 * ne), ("wb", ne)

    pieces = [(0, c) for c in [R] + L["direct"] + L["cross"]] + [(1, c) for c in L["cross"] + L["direct"] + [R]]
    P = len(pieces)
    zfree, zdone, relu, hq, yfin = {}, {}, {}, {}, {}

    def mm1(p, b):
        w, c = pieces[p]
        m, t, bank = wid[c], 5 * w + b, (4 * p + b) % NZ
        wait("pe", xarr[c] if c != R else qx, wall if w else qw[b])
        if bank in zfree:
            wait("pe", zfree[bank])
        zdone[(p, b)] = done("pe", g.tensor.matmul_mx(
            T.z[:, 512 * bank:512 * bank + m], T.wq[:, t * TW:(t + 1) * TW], T.ws[:, t * TW:(t + 1) * TW],
            T.xq[:, off[c]:off[c] + m], T.xs[:, off[c]:off[c] + m], True, True))

    def mm2(p):
        w, c = pieces[p]
        m, t, y = wid[c], 5 * w + 4, 512 * grp.index(c)
        wait("pe", hq[p], w2all if w else qw[4])
        yfin[p] = done("pe", g.tensor.matmul_mx(
            T.yp[:, y:y + m], T.wq[:, t * TW:(t + 1) * TW], T.ws[:, t * TW:(t + 1) * TW],
            T.hq[:, p * NC:p * NC + m], T.hs[:, p * NC:p * NC + m], w == 0, w == 1))

    def act(p, b):
        m, bank = wid[pieces[p][1]], (4 * p + b) % NZ
        out, src = T.h[:, 4 * NC * p + b:4 * NC * p + 4 * m:4], T.z[:, 512 * bank:512 * bank + m]
        if b in ((0, 1, 2) if p == 0 else (0, 2)):
            wait("ac", zdone[(p, b)])
            e = done("ac", g.scalar.activation(out, src, ActivationFunctionType.Relu, scale=C))
        else:
            wait("dv", zdone[(p, b)])
            e = done("dv", g.vector.tensor_scalar(out, src, 0.0, C, AluOpType.max, AluOpType.mult))
        relu[(p, b)] = zfree[bank] = e

    def quant(p):
        m = wid[pieces[p][1]]
        wait("dv", *[relu[(p, b)] for b in range(G)])
        hq[p] = done("dv", g.vector.quantize_mx(T.hq[:, p * NC:p * NC + m], T.hs[:, p * NC:p * NC + m],
                                                T.h[:, 4 * NC * p:4 * NC * p + 4 * m]))

    def ycopy(p):
        w, c = pieces[p]
        if w == 0 or c == R:
            return
        m, k = wid[c], grp.index(c)
        wait("ac", yfin[p])
        e = done("ac", g.scalar.activation(T.ysend[:, k * NC:k * NC + m], T.yp[:, 512 * k:512 * k + m], ActivationFunctionType.Copy))
        wait("g", e)
        src = T.ysend[:, k * NC:k * NC + m]
        if c in L["cross"]:
            send(relay("y", c, src, eon))
        else:
            send((c, src, T.yland[:, me * NC:me * NC + m], eoff, S["ya%d" % me]))

    for p in range(P):
        for b in range(G):
            mm1(p, b)
            act(p, b)
        if p:
            mm2(p - 1)
            ycopy(p - 1)
        quant(p)
    mm2(P - 1)

    first, last = (L["direct"] + L["cross"])[:2]
    wait("dv", yfin[P - 1], yarr[first])
    k = grp.index(first)
    e = done("dv", g.vector.tensor_tensor(T.yacc[:, :n], T.yp[:, 512 * me:512 * me + n], T.yland[:, k * NC:k * NC + n], AluOpType.add))
    wait("dv", e, yarr[last])
    k = grp.index(last)
    e = done("dv", g.vector.tensor_tensor(T.yout[:, :n], T.yacc[:, :n], T.yland[:, k * NC:k * NC + n], AluOpType.add))
    wait("sy", e)
    g.sync.dma_start(T.y[:, :n], T.yout[:, :n]).then_inc(S.st, 16)
    g.wait_ge(S.ls, sent[0])
    g.sync.wait_ge(S.st, 16)
